import numpy as np
CORES = [2,130,10,138,18,146,26,154,34,162,42,170,50,178,58,186]
N = 16
def setup_inputs(rng):
    return {"x": rng.standard_normal((N, 128, 256), dtype=np.float32)}
def reference(x):
    s = x.sum(axis=0, dtype=np.float64).astype(x.dtype)
    b = 256 // N
    return {"y": np.stack([s[:, r * b:(r + 1) * b] for r in range(N)])}

@@ -1,0 +1,89 @@
+from concourse.bass import DstId, RemoteDMATransfer
+
+B = 4
+A = 16 // B
+W = 256 // B
+RB = 2048 // B
+
+SCRATCH = {
+    "xs": ("dram", [2048, 16], "float32"),
+    "land": ("dram", [16, 128, 16], "float32"),
+    "res": ("dram", [128 * A, 16], "float32"),
+}
+SEMAPHORES = ["ld0", "ld1", "sent", "arr", "got", "st"]
+
+
+def _reducer(T, k):
+    return T.cores[k] + 1
+
+
+def _dst(topo, dst, src):
+    rid, pid = topo.addr(dst, src)
+    return DstId(rid=rid, pnc=pid)
+
+
+def _pieces(h):
+    if B == 1:
+        return [(0, 64 * h + 32 * t, 64 * h + 32 * t + 32) for t in range(2)]
+    if B == 2:
+        return [(h, 64 * t, 64 * t + 64) for t in range(2)]
+    return [(b, 0, 128) for b in range(h * B // 2, (h + 1) * B // 2)]
+
+
+def _rank(g, core, T, topo, rank):
+    order = [1 - rank // 8, rank // 8]
+    queues = [g.sync, g.scalar]
+    counts = []
+    for ph, h in enumerate(order):
+        ps = _pieces(h)
+        counts.append(16 * len(ps))
+        for i, (b, p0, p1) in enumerate(ps):
+            r0 = RB * b + p0 * W // 16
+            r1 = RB * b + p1 * W // 16
+            queues[i % 2].dma_start(T.xs[r0:r1, :], T.x[p0:p1, W * b:W * b + W]).then_inc(T.sem["ld%d" % ph], 16)
+    sent = 0
+    for ph, h in enumerate(order):
+        g.wait_ge(T.sem["ld%d" % ph], counts[ph])
+        trs = []
+        e = 0
+        for k in range(8 * h, 8 * h + 8):
+            if k == rank:
+                mask, n = 0xFF00, 8
+            else:
+                mask, n = 1 << e, 1
+                e += 1
+            sent += n
+            trs.append(RemoteDMATransfer(dst_ids=[_dst(topo, _reducer(T, k), core)], dma_engine_mask=mask,
+                                         remote_sem=T.sem.arr, src=T.xs[128 * k:128 * k + 128, :], dst=T.land[rank]))
+        g.remote_dma_fused(trs, local_sem=T.sem.sent)
+    m = rank % A
+    g.sync.wait_ge(T.sem.got, 8 * A)
+    g.sync.dma_start(T.y[:], T.res[m::A, :]).then_inc(T.sem.st, 16)
+    g.wait_ge(T.sem.sent, sent)
+    g.wait_ge(T.sem.got, 8 * A)
+    g.wait_ge(T.sem.st, 16)
+
+
+def _reduce(g, core, T, topo, k):
+    b, a = k // A, k % A
+    srcs = [T.land[s] for s in range(16)]
+    out = T.res[128 * a:128 * a + 128, :]
+    far = [A * b + i for i in range(A) if A * b + i != k]
+    trs = [RemoteDMATransfer(dst_ids=[_dst(topo, T.cores[k], core)], dma_engine_mask=0xFF00, remote_sem=T.sem.got,
+                             srcs=srcs, dsts=[out], alu_op=1)]
+    if far:
+        trs.append(RemoteDMATransfer(dst_ids=[_dst(topo, T.cores[r], core) for r in far], dma_engine_mask=0x00FF,
+                                     remote_sem=T.sem.got, srcs=srcs, dsts=[out for r in far], alu_op=1))
+    g.wait_ge(T.sem.arr, 15 + 8)
+    g.remote_dma_fused(trs, local_sem=T.sem.sent)
+    g.wait_ge(T.sem.sent, 8 * len(trs))
+
+
+def rank_program(g, core, T, topo):
+    rank = T.rank_of(core)
+    if rank is not None:
+        _rank(g, core, T, topo, rank)
+        return
+    k = T.rank_of(core - 1) if core % 8 == 3 else None
+    if k is not None:
+        _reduce(g, core, T, topo, k)

@@ -1,9 +1,10 @@
 from concourse.bass import DstId, RemoteDMATransfer
 
-B = 4
+B = 16
 A = 16 // B
 W = 256 // B
 RB = 2048 // B
+GOT = 16 if A == 1 else 8 * A
 
 SCRATCH = {
     "xs": ("dram", [2048, 16], "float32"),
@@ -57,10 +58,10 @@ def _rank(g, core, T, topo, rank):
                                          remote_sem=T.sem.arr, src=T.xs[128 * k:128 * k + 128, :], dst=T.land[rank]))
         g.remote_dma_fused(trs, local_sem=T.sem.sent)
     m = rank % A
-    g.sync.wait_ge(T.sem.got, 8 * A)
+    g.sync.wait_ge(T.sem.got, GOT)
     g.sync.dma_start(T.y[:], T.res[m::A, :]).then_inc(T.sem.st, 16)
     g.wait_ge(T.sem.sent, sent)
-    g.wait_ge(T.sem.got, 8 * A)
+    g.wait_ge(T.sem.got, GOT)
     g.wait_ge(T.sem.st, 16)
 
 
@@ -69,14 +70,14 @@ def _reduce(g, core, T, topo, k):
     srcs = [T.land[s] for s in range(16)]
     out = T.res[128 * a:128 * a + 128, :]
     far = [A * b + i for i in range(A) if A * b + i != k]
-    trs = [RemoteDMATransfer(dst_ids=[_dst(topo, T.cores[k], core)], dma_engine_mask=0xFF00, remote_sem=T.sem.got,
-                             srcs=srcs, dsts=[out], alu_op=1)]
+    trs = [RemoteDMATransfer(dst_ids=[_dst(topo, T.cores[k], core)], dma_engine_mask=0xFF00 if far else 0xFFFF,
+                             remote_sem=T.sem.got, srcs=srcs, dsts=[out], alu_op=1)]
     if far:
         trs.append(RemoteDMATransfer(dst_ids=[_dst(topo, T.cores[r], core) for r in far], dma_engine_mask=0x00FF,
                                      remote_sem=T.sem.got, srcs=srcs, dsts=[out for r in far], alu_op=1))
     g.wait_ge(T.sem.arr, 15 + 8)
     g.remote_dma_fused(trs, local_sem=T.sem.sent)
-    g.wait_ge(T.sem.sent, 8 * len(trs))
+    g.wait_ge(T.sem.sent, 16)
 
 
 def rank_program(g, core, T, topo):

@@ -1,21 +1,13 @@
 from concourse.bass import DstId, RemoteDMATransfer
 
-B = 16
-A = 16 // B
-W = 256 // B
-RB = 2048 // B
-GOT = 16 if A == 1 else 8 * A
+PHASES = [[2], [1, 3], [0]]
 
 SCRATCH = {
     "xs": ("dram", [2048, 16], "float32"),
     "land": ("dram", [16, 128, 16], "float32"),
-    "res": ("dram", [128 * A, 16], "float32"),
+    "res": ("dram", [128, 16], "float32"),
 }
-SEMAPHORES = ["ld0", "ld1", "sent", "arr", "got", "st"]
-
-
-def _reducer(T, k):
-    return T.cores[k] + 1
+SEMAPHORES = ["ld%d" % i for i in range(len(PHASES))] + ["sent", "arr", "got", "st"]
 
 
 def _dst(topo, dst, src):
@@ -23,60 +15,49 @@ def _dst(topo, dst, src):
     return DstId(rid=rid, pnc=pid)
 
 
-def _pieces(h):
-    if B == 1:
-        return [(0, 64 * h + 32 * t, 64 * h + 32 * t + 32) for t in range(2)]
-    if B == 2:
-        return [(h, 64 * t, 64 * t + 64) for t in range(2)]
-    return [(b, 0, 128) for b in range(h * B // 2, (h + 1) * B // 2)]
+def _engines(off):
+    for ph in PHASES:
+        if off in ph:
+            return 2 // len(ph)
 
 
 def _rank(g, core, T, topo, rank):
-    order = [1 - rank // 8, rank // 8]
+    q = rank // 4
+    groups = [[4 * ((q + off) % 4) + i for off in ph for i in range(4)] for ph in PHASES]
     queues = [g.sync, g.scalar]
-    counts = []
-    for ph, h in enumerate(order):
-        ps = _pieces(h)
-        counts.append(16 * len(ps))
-        for i, (b, p0, p1) in enumerate(ps):
-            r0 = RB * b + p0 * W // 16
-            r1 = RB * b + p1 * W // 16
-            queues[i % 2].dma_start(T.xs[r0:r1, :], T.x[p0:p1, W * b:W * b + W]).then_inc(T.sem["ld%d" % ph], 16)
+    for ph, tiles in enumerate(groups):
+        for i, k in enumerate(tiles):
+            queues[i % 2].dma_start(T.xs[128 * k:128 * k + 128, :],
+                                    T.x[:, 16 * k:16 * k + 16]).then_inc(T.sem["ld%d" % ph], 16)
     sent = 0
-    for ph, h in enumerate(order):
-        g.wait_ge(T.sem["ld%d" % ph], counts[ph])
+    for ph, tiles in enumerate(groups):
+        ne = 8 // len(tiles)
         trs = []
         e = 0
-        for k in range(8 * h, 8 * h + 8):
+        for k in tiles:
             if k == rank:
                 mask, n = 0xFF00, 8
             else:
-                mask, n = 1 << e, 1
-                e += 1
+                mask, n = ((1 << ne) - 1) << e, ne
+                e += ne
             sent += n
-            trs.append(RemoteDMATransfer(dst_ids=[_dst(topo, _reducer(T, k), core)], dma_engine_mask=mask,
+            trs.append(RemoteDMATransfer(dst_ids=[_dst(topo, T.cores[k] + 1, core)], dma_engine_mask=mask,
                                          remote_sem=T.sem.arr, src=T.xs[128 * k:128 * k + 128, :], dst=T.land[rank]))
+        g.wait_ge(T.sem["ld%d" % ph], 16 * len(tiles))
         g.remote_dma_fused(trs, local_sem=T.sem.sent)
-    m = rank % A
-    g.sync.wait_ge(T.sem.got, GOT)
-    g.sync.dma_start(T.y[:], T.res[m::A, :]).then_inc(T.sem.st, 16)
+    g.sync.wait_ge(T.sem.got, 16)
+    g.sync.dma_start(T.y[:], T.res[:]).then_inc(T.sem.st, 16)
     g.wait_ge(T.sem.sent, sent)
-    g.wait_ge(T.sem.got, GOT)
+    g.wait_ge(T.sem.got, 16)
     g.wait_ge(T.sem.st, 16)
 
 
 def _reduce(g, core, T, topo, k):
-    b, a = k // A, k % A
-    srcs = [T.land[s] for s in range(16)]
-    out = T.res[128 * a:128 * a + 128, :]
-    far = [A * b + i for i in range(A) if A * b + i != k]
-    trs = [RemoteDMATransfer(dst_ids=[_dst(topo, T.cores[k], core)], dma_engine_mask=0xFF00 if far else 0xFFFF,
-                             remote_sem=T.sem.got, srcs=srcs, dsts=[out], alu_op=1)]
-    if far:
-        trs.append(RemoteDMATransfer(dst_ids=[_dst(topo, T.cores[r], core) for r in far], dma_engine_mask=0x00FF,
-                                     remote_sem=T.sem.got, srcs=srcs, dsts=[out for r in far], alu_op=1))
-    g.wait_ge(T.sem.arr, 15 + 8)
-    g.remote_dma_fused(trs, local_sem=T.sem.sent)
+    tr = RemoteDMATransfer(dst_ids=[_dst(topo, T.cores[k], core)], dma_engine_mask=0xFFFF, remote_sem=T.sem.got,
+                           srcs=[T.land[s] for s in range(16)], dsts=[T.res[:]], alu_op=1)
+    arrive = 8 + sum(_engines((k // 4 - s // 4) % 4) for s in range(16) if s != k)
+    g.wait_ge(T.sem.arr, arrive)
+    g.remote_dma_fused([tr], local_sem=T.sem.sent)
     g.wait_ge(T.sem.sent, 16)
 
 

@@ -1,6 +1,11 @@
 from concourse.bass import DstId, RemoteDMATransfer
 
-PHASES = [[2], [1, 3], [0]]
+PHASES = [
+    [(2, 1, 0, 2), (2, 1, 1, 2), (1, 1, 0, 2), (1, 1, 1, 2)],
+    [(3, 1, 0, 1), (3, 1, 1, 1), (0, 1, 1, 1), (2, 0, 0, 1), (2, 0, 1, 1), (1, 0, 0, 1), (1, 0, 1, 1), (3, 0, 0, 1)],
+    [(3, 0, 1, 2), (0, 0, 1, 2), (0, 1, 0, 4), (0, 0, 0, 8)],
+]
+ARRIVE = sum(n for ph in PHASES for (dj, dp, dh, n) in ph)
 
 SCRATCH = {
     "xs": ("dram", [2048, 16], "float32"),
@@ -15,39 +20,30 @@ def _dst(topo, dst, src):
     return DstId(rid=rid, pnc=pid)
 
 
-def _engines(off):
-    for ph in PHASES:
-        if off in ph:
-            return 2 // len(ph)
-
-
 def _rank(g, core, T, topo, rank):
-    q = rank // 4
-    groups = [[4 * ((q + off) % 4) + i for off in ph for i in range(4)] for ph in PHASES]
+    j, p, h = rank // 4, (rank // 2) % 2, rank % 2
+    groups = [[(4 * ((j + dj) % 4) + 2 * (p ^ dp) + (h ^ dh), n) for (dj, dp, dh, n) in ph] for ph in PHASES]
     queues = [g.sync, g.scalar]
     for ph, tiles in enumerate(groups):
-        for i, k in enumerate(tiles):
+        for i, (k, n) in enumerate(tiles):
             queues[i % 2].dma_start(T.xs[128 * k:128 * k + 128, :],
                                     T.x[:, 16 * k:16 * k + 16]).then_inc(T.sem["ld%d" % ph], 16)
-    sent = 0
     for ph, tiles in enumerate(groups):
-        ne = 8 // len(tiles)
         trs = []
         e = 0
-        for k in tiles:
+        for k, n in tiles:
             if k == rank:
-                mask, n = 0xFF00, 8
+                mask = 0xFF00
             else:
-                mask, n = ((1 << ne) - 1) << e, ne
-                e += ne
-            sent += n
+                mask = ((1 << n) - 1) << e
+                e += n
             trs.append(RemoteDMATransfer(dst_ids=[_dst(topo, T.cores[k] + 1, core)], dma_engine_mask=mask,
                                          remote_sem=T.sem.arr, src=T.xs[128 * k:128 * k + 128, :], dst=T.land[rank]))
         g.wait_ge(T.sem["ld%d" % ph], 16 * len(tiles))
         g.remote_dma_fused(trs, local_sem=T.sem.sent)
     g.sync.wait_ge(T.sem.got, 16)
     g.sync.dma_start(T.y[:], T.res[:]).then_inc(T.sem.st, 16)
-    g.wait_ge(T.sem.sent, sent)
+    g.wait_ge(T.sem.sent, ARRIVE)
     g.wait_ge(T.sem.got, 16)
     g.wait_ge(T.sem.st, 16)
 
@@ -55,8 +51,7 @@ def _rank(g, core, T, topo, rank):
 def _reduce(g, core, T, topo, k):
     tr = RemoteDMATransfer(dst_ids=[_dst(topo, T.cores[k], core)], dma_engine_mask=0xFFFF, remote_sem=T.sem.got,
                            srcs=[T.land[s] for s in range(16)], dsts=[T.res[:]], alu_op=1)
-    arrive = 8 + sum(_engines((k // 4 - s // 4) % 4) for s in range(16) if s != k)
-    g.wait_ge(T.sem.arr, arrive)
+    g.wait_ge(T.sem.arr, ARRIVE)
     g.remote_dma_fused([tr], local_sem=T.sem.sent)
     g.wait_ge(T.sem.sent, 16)
 

from concourse.bass import DstId, RemoteDMATransfer

PHASES = [
    [(2, 1, 0, 2), (2, 1, 1, 2), (1, 1, 0, 2), (1, 1, 1, 2)],
    [(3, 1, 0, 1), (3, 1, 1, 1), (0, 1, 1, 1), (2, 0, 0, 1), (2, 0, 1, 1), (1, 0, 0, 1), (1, 0, 1, 1), (3, 0, 0, 1)],
    [(3, 0, 1, 2), (0, 0, 1, 2), (0, 1, 0, 4), (0, 0, 0, 8)],
]
ARRIVE = sum(n for ph in PHASES for (dj, dp, dh, n) in ph)

SCRATCH = {
    "xs": ("dram", [2048, 16], "float32"),
    "land": ("dram", [16, 128, 16], "float32"),
    "res": ("dram", [128, 16], "float32"),
}
SEMAPHORES = ["ld%d" % i for i in range(len(PHASES))] + ["sent", "arr", "got", "st"]


def _dst(topo, dst, src):
    rid, pid = topo.addr(dst, src)
    return DstId(rid=rid, pnc=pid)


def _rank(g, core, T, topo, rank):
    j, p, h = rank // 4, (rank // 2) % 2, rank % 2
    groups = [[(4 * ((j + dj) % 4) + 2 * (p ^ dp) + (h ^ dh), n) for (dj, dp, dh, n) in ph] for ph in PHASES]
    queues = [g.sync, g.scalar]
    for ph, tiles in enumerate(groups):
        for i, (k, n) in enumerate(tiles):
            queues[i % 2].dma_start(T.xs[128 * k:128 * k + 128, :],
                                    T.x[:, 16 * k:16 * k + 16]).then_inc(T.sem["ld%d" % ph], 16)
    for ph, tiles in enumerate(groups):
        trs = []
        e = 0
        for k, n in tiles:
            if k == rank:
                mask = 0xFF00
            else:
                mask = ((1 << n) - 1) << e
                e += n
            trs.append(RemoteDMATransfer(dst_ids=[_dst(topo, T.cores[k] + 1, core)], dma_engine_mask=mask,
                                         remote_sem=T.sem.arr, src=T.xs[128 * k:128 * k + 128, :], dst=T.land[rank]))
        g.wait_ge(T.sem["ld%d" % ph], 16 * len(tiles))
        g.remote_dma_fused(trs, local_sem=T.sem.sent)
    g.sync.wait_ge(T.sem.got, 16)
    g.sync.dma_start(T.y[:], T.res[:]).then_inc(T.sem.st, 16)
    g.wait_ge(T.sem.sent, ARRIVE)
    g.wait_ge(T.sem.got, 16)
    g.wait_ge(T.sem.st, 16)


def _reduce(g, core, T, topo, k):
    tr = RemoteDMATransfer(dst_ids=[_dst(topo, T.cores[k], core)], dma_engine_mask=0xFFFF, remote_sem=T.sem.got,
                           srcs=[T.land[s] for s in range(16)], dsts=[T.res[:]], alu_op=1)
    g.wait_ge(T.sem.arr, ARRIVE)
    g.remote_dma_fused([tr], local_sem=T.sem.sent)
    g.wait_ge(T.sem.sent, 16)


def rank_program(g, core, T, topo):
    rank = T.rank_of(core)
    if rank is not None:
        _rank(g, core, T, topo, rank)
        return
    k = T.rank_of(core - 1) if core % 8 == 3 else None
    if k is not None:
        _reduce(g, core, T, topo, k)
